import numpy as np
import ml_dtypes


def mxq(x, axis, fmt="e4m3"):
    dtype, down = {"e4m3": (ml_dtypes.float8_e4m3fn, 7), "e5m2": (ml_dtypes.float8_e5m2, 14)}[fmt]
    v = np.moveaxis(np.asarray(x, np.float32).astype(ml_dtypes.bfloat16).astype(np.float64), axis, -1)
    blocks = v.reshape(v.shape[:-1] + (-1, 32))
    amax = np.abs(blocks).max(-1, keepdims=True)
    byte = np.maximum(np.where(amax > 0, np.frexp(amax)[1] - 1 + 127, 0) - down, 1)
    scale = np.exp2(byte - 127.0)
    codes = (blocks / scale).astype(np.float32).astype(dtype).astype(np.float64)
    return np.moveaxis((codes * scale).reshape(v.shape), -1, axis)


WIDE = False


def mx_kscale(k):
    if not WIDE:
        return np.ones(k)
    levels = np.array([10, -10, 5, -5, 0])
    if k % 512:
        return np.exp2(np.random.permutation(np.resize(levels, k // 32))).repeat(32)
    a = np.empty((k // 512, 16))
    for p in range(k // 512):
        a[p, :8] = np.random.permutation(np.resize(levels, 8))
        for g in range(8):
            far = levels[np.abs(levels - a[p, g]) >= 10]
            a[p, g + 8] = far[np.random.randint(len(far))]
    return np.exp2(a.ravel()).repeat(32)


def f64(x):
    return np.asarray(x).astype(np.float64)


def striped(idx):
    return np.tile(np.asarray(idx).reshape(-1, 16).T, (8, 1)).astype(np.uint16)


def unstriped(offs):
    return offs[:16].T.reshape(-1).astype(np.int64)


B, N, T, D, DV, NQ = 2, 512, 2048, 512, 256, 128
PAGE = 64


def setup_inputs():
    n = np.random.standard_normal
    pages = np.random.permutation(T // PAGE)[:B * N // PAGE]
    idx = (pages[:, None] * PAGE + np.arange(PAGE)[None, :]).reshape(-1)
    u = mx_kscale(B * N)
    ut = np.ones(T)
    ut[idx] = u
    w = np.exp(n((B, N, NQ)))
    w = w / w.sum(1, keepdims=True)
    return {
        "wT": (w * u.reshape(B, N, 1)).astype(np.float32),
        "vT": (n((DV, T)) / ut).astype(np.float32),
        "offs": striped(idx),
    }


def reference(wT, vT, offs):
    idx = unstriped(offs)
    pick = lambda x: x[:, idx].reshape(x.shape[0], B, N).transpose(1, 0, 2)
    return mxq(f64(wT), 1, "e4m3").transpose(0, 2, 1) @ mxq(pick(f64(vT)).transpose(0, 2, 1), 1, "e4m3")

@@ -1,0 +1,118 @@
+from contextlib import ExitStack
+
+import concourse.mybir as mybir
+from concourse.masks import make_identity
+
+B, N, T, DV, NQ = 2, 512, 2048, 256, 128
+FLOPS = 2 * B * N * NQ * DV
+
+F32 = mybir.dt.float32
+BF16 = mybir.dt.bfloat16
+U32 = mybir.dt.uint32
+U16 = mybir.dt.uint16
+U8 = mybir.dt.uint8
+FP8X4 = mybir.dt.float8_e4m3fn_x4
+
+P = 128
+PACK = 4
+BLOCKS = DV // P
+COLS = N // 16
+
+
+def tile_attend_spmm_kernel(tc, wT, vT, offs, out):
+    nc = tc.nc
+    with ExitStack() as ctx:
+        keep = ctx.enter_context(tc.tile_pool(name="keep", bufs=1))
+        turn = ctx.enter_context(tc.psum_pool(name="turn", bufs=2))
+        psum = ctx.enter_context(tc.psum_pool(name="psum", bufs=1))
+
+        offsets = keep.tile([P, B * COLS], U16, name="offsets")
+        nc.sync.dma_start(offsets[:], offs)
+
+        pool_tiles = []
+        for b in range(BLOCKS):
+            values = keep.tile([P, T], F32, name=f"values{b}")
+            nc.sync.dma_start(out=values[:], in_=vT[b * P : (b + 1) * P, :])
+            pool_tiles.append(values)
+
+        w_raw = []
+        for s in range(B):
+            raw = keep.tile([P, PACK, NQ], F32, name=f"w_raw{s}")
+            nc.sync.dma_start(out=raw[:], in_=wT[s].rearrange("(p j) q -> p j q", j=PACK))
+            w_raw.append(raw)
+
+        identity = keep.tile([P, P], F32, name="identity")
+        make_identity(nc, identity[:])
+
+        v_codes = [keep.tile([P, DV], U32, align_bytes=64, name=f"v_codes{s}") for s in range(B)]
+        v_scales = [keep.tile([P, DV], U8, align_bytes=64, name=f"v_scales{s}") for s in range(B)]
+        w_codes = [keep.tile([P, NQ], U32, align_bytes=64, name=f"w_codes{s}") for s in range(B)]
+        w_scales = [keep.tile([P, NQ], U8, align_bytes=64, name=f"w_scales{s}") for s in range(B)]
+        grouped = {}
+
+        def gather(b, s):
+            picked = keep.tile([P, 2, P, 2], BF16, align_bytes=64, name=f"picked{b}{s}")
+            nc.vector.tensor_copy(
+                picked[:].rearrange("p u s v -> p s u v"),
+                pool_tiles[b][:].indirect(offsets[:, s * COLS : (s + 1) * COLS]),
+            )
+            words = picked[:].rearrange("p u s v -> p (u s v)").bitcast(F32)
+            turned = turn.tile([P, 2, P], F32, name="turned")
+            for u in range(2):
+                nc.tensor.transpose(turned[:, u, :], words[:, u * P : (u + 1) * P], identity[:])
+            g = keep.tile([P, P, PACK], BF16, align_bytes=64, name=f"grouped{b}{s}")
+            nc.scalar.copy(
+                out=g[:].rearrange("p e j -> p (e j)").bitcast(F32).rearrange("p (e u) -> p e u", u=2),
+                in_=turned[:].rearrange("p u e -> p e u"),
+            )
+            grouped[b, s] = g
+
+        def quantize(b, s):
+            cols = slice(b * P, (b + 1) * P)
+            nc.vector.quantize_mx(
+                out=v_codes[s][:, cols].bitcast(FP8X4),
+                scales=v_scales[s][:, cols],
+                in_=grouped[b, s][:].rearrange("p e j -> p (e j)"),
+            )
+
+        w_grouped = [keep.tile([P, NQ, PACK], BF16, align_bytes=64, name=f"w_grouped{s}") for s in range(B)]
+
+        def quantize_weights(s):
+            nc.vector.quantize_mx(
+                out=w_codes[s][:].bitcast(FP8X4),
+                scales=w_scales[s][:],
+                in_=w_grouped[s][:].rearrange("p q j -> p (q j)"),
+            )
+
+        gather(0, 0)
+        gather(0, 1)
+        quantize(0, 0)
+        quantize(0, 1)
+        gather(1, 0)
+        gather(1, 1)
+        nc.scalar.copy(out=w_grouped[0][:], in_=w_raw[0][:].rearrange("p j q -> p q j"))
+        nc.vector.tensor_copy(out=w_grouped[1][:], in_=w_raw[1][:].rearrange("p j q -> p q j"))
+        quantize(1, 0)
+        quantize_weights(0)
+        quantize_weights(1)
+        quantize(1, 1)
+
+        for s in range(B):
+            result = keep.tile([NQ, DV], F32, name=f"result{s}")
+            for b in range(BLOCKS):
+                cols = slice(b * P, (b + 1) * P)
+                acc = psum.tile([NQ, P], F32, name=f"acc{s}{b}")
+                nc.tensor.matmul_mx(
+                    out=acc[:],
+                    lhsT=w_codes[s][:].bitcast(FP8X4),
+                    lhsT_scale=w_scales[s][:],
+                    rhs=v_codes[s][:, cols].bitcast(FP8X4),
+                    rhs_scale=v_scales[s][:, cols],
+                    start=True,
+                    stop=True,
+                )
+                if b == 0:
+                    nc.vector.tensor_copy(out=result[:, cols], in_=acc[:])
+                else:
+                    nc.scalar.copy(out=result[:, cols], in_=acc[:])
+            nc.sync.dma_start(out=out[s], in_=result[:])

@@ -32,13 +32,17 @@ def tile_attend_spmm_kernel(tc, wT, vT, offs, out):
         pool_tiles = []
         for b in range(BLOCKS):
             values = keep.tile([P, T], F32, name=f"values{b}")
-            nc.sync.dma_start(out=values[:], in_=vT[b * P : (b + 1) * P, :])
+            half = T // 2
+            rows = slice(b * P, (b + 1) * P)
+            nc.scalar.dma_start(out=values[:, 0:half], in_=vT[rows, 0:half])
+            nc.sync.dma_start(out=values[:, half:T], in_=vT[rows, half:T])
             pool_tiles.append(values)
 
         w_raw = []
         for s in range(B):
             raw = keep.tile([P, PACK, NQ], F32, name=f"w_raw{s}")
-            nc.sync.dma_start(out=raw[:], in_=wT[s].rearrange("(p j) q -> p j q", j=PACK))
+            queue = nc.scalar if s == 0 else nc.sync
+            queue.dma_start(out=raw[:], in_=wT[s].rearrange("(p j) q -> p j q", j=PACK))
             w_raw.append(raw)
 
         identity = keep.tile([P, P], F32, name="identity")

@@ -23,45 +23,36 @@ def tile_attend_spmm_kernel(tc, wT, vT, offs, out):
     nc = tc.nc
     with ExitStack() as ctx:
         keep = ctx.enter_context(tc.tile_pool(name="keep", bufs=1))
-        turn = ctx.enter_context(tc.psum_pool(name="turn", bufs=2))
         psum = ctx.enter_context(tc.psum_pool(name="psum", bufs=1))
 
         offsets = keep.tile([P, B * COLS], U16, name="offsets")
         nc.sync.dma_start(offsets[:], offs)
 
-        pool_tiles = []
-        for b in range(BLOCKS):
-            values = keep.tile([P, T], F32, name=f"values{b}")
-            half = T // 2
-            rows = slice(b * P, (b + 1) * P)
-            nc.scalar.dma_start(out=values[:, 0:half], in_=vT[rows, 0:half])
-            nc.sync.dma_start(out=values[:, half:T], in_=vT[rows, half:T])
-            pool_tiles.append(values)
-
-        w_raw = []
-        for s in range(B):
-            raw = keep.tile([P, PACK, NQ], F32, name=f"w_raw{s}")
-            queue = nc.scalar if s == 0 else nc.sync
-            queue.dma_start(out=raw[:], in_=wT[s].rearrange("(p j) q -> p j q", j=PACK))
-            w_raw.append(raw)
+        values = [keep.tile([P, T], F32, name=f"values{b}") for b in range(BLOCKS)]
+        w_raw = [keep.tile([P, PACK, NQ], F32, name=f"w_raw{s}") for s in range(B)]
+        nc.sync.dma_start(out=values[0][:], in_=vT[0 * P : 1 * P, :])
+        nc.sync.dma_start(out=values[1][:], in_=vT[1 * P : 2 * P, :])
+        nc.sync.dma_start(out=w_raw[0][:], in_=wT[0].rearrange("(p j) q -> p j q", j=PACK))
+        nc.sync.dma_start(out=w_raw[1][:], in_=wT[1].rearrange("(p j) q -> p j q", j=PACK))
 
         identity = keep.tile([P, P], F32, name="identity")
         make_identity(nc, identity[:])
 
-        v_codes = [keep.tile([P, DV], U32, align_bytes=64, name=f"v_codes{s}") for s in range(B)]
-        v_scales = [keep.tile([P, DV], U8, align_bytes=64, name=f"v_scales{s}") for s in range(B)]
+        v_codes = [[keep.tile([P, P], U32, align_bytes=64, name=f"v_codes{s}{b}") for b in range(BLOCKS)] for s in range(B)]
+        v_scales = [[keep.tile([P, P], U8, align_bytes=64, name=f"v_scales{s}{b}") for b in range(BLOCKS)] for s in range(B)]
         w_codes = [keep.tile([P, NQ], U32, align_bytes=64, name=f"w_codes{s}") for s in range(B)]
         w_scales = [keep.tile([P, NQ], U8, align_bytes=64, name=f"w_scales{s}") for s in range(B)]
+        w_grouped = [keep.tile([P, NQ, PACK], BF16, align_bytes=64, name=f"w_grouped{s}") for s in range(B)]
         grouped = {}
 
         def gather(b, s):
             picked = keep.tile([P, 2, P, 2], BF16, align_bytes=64, name=f"picked{b}{s}")
             nc.vector.tensor_copy(
                 picked[:].rearrange("p u s v -> p s u v"),
-                pool_tiles[b][:].indirect(offsets[:, s * COLS : (s + 1) * COLS]),
+                values[b][:].indirect(offsets[:, s * COLS : (s + 1) * COLS]),
             )
             words = picked[:].rearrange("p u s v -> p (u s v)").bitcast(F32)
-            turned = turn.tile([P, 2, P], F32, name="turned")
+            turned = psum.tile([P, 2, P], F32, name=f"turned{b}{s}")
             for u in range(2):
                 nc.tensor.transpose(turned[:, u, :], words[:, u * P : (u + 1) * P], identity[:])
             g = keep.tile([P, P, PACK], BF16, align_bytes=64, name=f"grouped{b}{s}")
@@ -72,14 +63,11 @@ def tile_attend_spmm_kernel(tc, wT, vT, offs, out):
             grouped[b, s] = g
 
         def quantize(b, s):
-            cols = slice(b * P, (b + 1) * P)
             nc.vector.quantize_mx(
-                out=v_codes[s][:, cols].bitcast(FP8X4),
-                scales=v_scales[s][:, cols],
+                out=v_codes[s][b][:].bitcast(FP8X4),
+                scales=v_scales[s][b][:],
                 in_=grouped[b, s][:].rearrange("p e j -> p (e j)"),
             )
-
-        w_grouped = [keep.tile([P, NQ, PACK], BF16, align_bytes=64, name=f"w_grouped{s}") for s in range(B)]
 
         def quantize_weights(s):
             nc.vector.quantize_mx(
@@ -88,35 +76,55 @@ def tile_attend_spmm_kernel(tc, wT, vT, offs, out):
                 in_=w_grouped[s][:].rearrange("p q j -> p (q j)"),
             )
 
+        def round_scalar(s):
+            nc.scalar.copy(out=w_grouped[s][:], in_=w_raw[s][:].rearrange("p j q -> p q j"))
+
+        def round_vector(s):
+            nc.vector.tensor_copy(out=w_grouped[s][:], in_=w_raw[s][:].rearrange("p j q -> p q j"))
+
+        result = [keep.tile([NQ, DV], F32, name=f"result{s}") for s in range(B)]
+
+        def multiply(s, b):
+            acc = psum.tile([NQ, P], F32, name=f"acc{s}{b}")
+            nc.tensor.matmul_mx(
+                out=acc[:],
+                lhsT=w_codes[s][:].bitcast(FP8X4),
+                lhsT_scale=w_scales[s][:],
+                rhs=v_codes[s][b][:].bitcast(FP8X4),
+                rhs_scale=v_scales[s][b][:],
+                start=True,
+                stop=True,
+            )
+            return acc
+
+        def finish_scalar(s, b, acc):
+            nc.scalar.copy(out=result[s][:, b * P : (b + 1) * P], in_=acc[:])
+
+        def finish_vector(s, b, acc):
+            nc.vector.tensor_copy(out=result[s][:, b * P : (b + 1) * P], in_=acc[:])
+
+        def store(s):
+            nc.sync.dma_start(out=out[s], in_=result[s][:])
+
         gather(0, 0)
         gather(0, 1)
         quantize(0, 0)
         quantize(0, 1)
         gather(1, 0)
         gather(1, 1)
-        nc.scalar.copy(out=w_grouped[0][:], in_=w_raw[0][:].rearrange("p j q -> p q j"))
-        nc.vector.tensor_copy(out=w_grouped[1][:], in_=w_raw[1][:].rearrange("p j q -> p q j"))
+        round_scalar(0)
+        round_vector(1)
         quantize(1, 0)
         quantize_weights(0)
         quantize_weights(1)
         quantize(1, 1)
-
-        for s in range(B):
-            result = keep.tile([NQ, DV], F32, name=f"result{s}")
-            for b in range(BLOCKS):
-                cols = slice(b * P, (b + 1) * P)
-                acc = psum.tile([NQ, P], F32, name=f"acc{s}{b}")
-                nc.tensor.matmul_mx(
-                    out=acc[:],
-                    lhsT=w_codes[s][:].bitcast(FP8X4),
-                    lhsT_scale=w_scales[s][:],
-                    rhs=v_codes[s][:, cols].bitcast(FP8X4),
-                    rhs_scale=v_scales[s][:, cols],
-                    start=True,
-                    stop=True,
-                )
-                if b == 0:
-                    nc.vector.tensor_copy(out=result[:, cols], in_=acc[:])
-                else:
-                    nc.scalar.copy(out=result[:, cols], in_=acc[:])
-            nc.sync.dma_start(out=out[s], in_=result[:])
+        a00 = multiply(0, 0)
+        a01 = multiply(0, 1)
+        a10 = multiply(1, 0)
+        a11 = multiply(1, 1)
+        finish_scalar(0, 0, a00)
+        finish_scalar(0, 1, a01)
+        store(0)
+        finish_scalar(1, 0, a10)
+        finish_vector(1, 1, a11)
+        store(1)

@@ -45,12 +45,21 @@ def tile_attend_spmm_kernel(tc, wT, vT, offs, out):
         w_grouped = [keep.tile([P, NQ, PACK], BF16, align_bytes=64, name=f"w_grouped{s}") for s in range(B)]
         grouped = {}
 
+        rounded0 = keep.tile([P, T], BF16, align_bytes=64, name="rounded0")
+
+        def round_values():
+            split = 1024
+            nc.vector.tensor_copy(out=rounded0[:, 0:split], in_=values[0][:, 0:split])
+            nc.scalar.copy(out=rounded0[:, split:T], in_=values[0][:, split:T])
+
         def gather(b, s):
             picked = keep.tile([P, 2, P, 2], BF16, align_bytes=64, name=f"picked{b}{s}")
-            nc.vector.tensor_copy(
-                picked[:].rearrange("p u s v -> p s u v"),
-                values[b][:].indirect(offsets[:, s * COLS : (s + 1) * COLS]),
-            )
+            listed = offsets[:, s * COLS : (s + 1) * COLS]
+            by_slot = picked[:].rearrange("p u s v -> p s u v")
+            if (b, s) == (0, 1):
+                nc.scalar.activation(by_slot, rounded0[:].indirect(listed), mybir.ActivationFunctionType.Copy)
+            else:
+                nc.vector.tensor_copy(by_slot, values[b][:].indirect(listed))
             words = picked[:].rearrange("p u s v -> p (u s v)").bitcast(F32)
             turned = psum.tile([P, 2, P], F32, name=f"turned{b}{s}")
             for u in range(2):
@@ -106,14 +115,15 @@ def tile_attend_spmm_kernel(tc, wT, vT, offs, out):
         def store(s):
             nc.sync.dma_start(out=out[s], in_=result[s][:])
 
+        round_values()
         gather(0, 0)
         gather(0, 1)
-        quantize(0, 0)
-        quantize(0, 1)
         gather(1, 0)
         gather(1, 1)
         round_scalar(0)
         round_vector(1)
+        quantize(0, 0)
+        quantize(0, 1)
         quantize(1, 0)
         quantize_weights(0)
         quantize_weights(1)

from contextlib import ExitStack

import concourse.mybir as mybir
from concourse.masks import make_identity

B, N, T, DV, NQ = 2, 512, 2048, 256, 128
FLOPS = 2 * B * N * NQ * DV

F32 = mybir.dt.float32
BF16 = mybir.dt.bfloat16
U32 = mybir.dt.uint32
U16 = mybir.dt.uint16
U8 = mybir.dt.uint8
FP8X4 = mybir.dt.float8_e4m3fn_x4

P = 128
PACK = 4
BLOCKS = DV // P
COLS = N // 16


def tile_attend_spmm_kernel(tc, wT, vT, offs, out):
    nc = tc.nc
    with ExitStack() as ctx:
        keep = ctx.enter_context(tc.tile_pool(name="keep", bufs=1))
        psum = ctx.enter_context(tc.psum_pool(name="psum", bufs=1))

        offsets = keep.tile([P, B * COLS], U16, name="offsets")
        nc.sync.dma_start(offsets[:], offs)

        values = [keep.tile([P, T], F32, name=f"values{b}") for b in range(BLOCKS)]
        w_raw = [keep.tile([P, PACK, NQ], F32, name=f"w_raw{s}") for s in range(B)]
        nc.sync.dma_start(out=values[0][:], in_=vT[0 * P : 1 * P, :])
        nc.sync.dma_start(out=values[1][:], in_=vT[1 * P : 2 * P, :])
        nc.sync.dma_start(out=w_raw[0][:], in_=wT[0].rearrange("(p j) q -> p j q", j=PACK))
        nc.sync.dma_start(out=w_raw[1][:], in_=wT[1].rearrange("(p j) q -> p j q", j=PACK))

        identity = keep.tile([P, P], F32, name="identity")
        make_identity(nc, identity[:])

        v_codes = [[keep.tile([P, P], U32, align_bytes=64, name=f"v_codes{s}{b}") for b in range(BLOCKS)] for s in range(B)]
        v_scales = [[keep.tile([P, P], U8, align_bytes=64, name=f"v_scales{s}{b}") for b in range(BLOCKS)] for s in range(B)]
        w_codes = [keep.tile([P, NQ], U32, align_bytes=64, name=f"w_codes{s}") for s in range(B)]
        w_scales = [keep.tile([P, NQ], U8, align_bytes=64, name=f"w_scales{s}") for s in range(B)]
        w_grouped = [keep.tile([P, NQ, PACK], BF16, align_bytes=64, name=f"w_grouped{s}") for s in range(B)]
        grouped = {}

        rounded0 = keep.tile([P, T], BF16, align_bytes=64, name="rounded0")

        def round_values():
            split = 1024
            nc.vector.tensor_copy(out=rounded0[:, 0:split], in_=values[0][:, 0:split])
            nc.scalar.copy(out=rounded0[:, split:T], in_=values[0][:, split:T])

        def gather(b, s):
            picked = keep.tile([P, 2, P, 2], BF16, align_bytes=64, name=f"picked{b}{s}")
            listed = offsets[:, s * COLS : (s + 1) * COLS]
            by_slot = picked[:].rearrange("p u s v -> p s u v")
            if (b, s) == (0, 1):
                nc.scalar.activation(by_slot, rounded0[:].indirect(listed), mybir.ActivationFunctionType.Copy)
            else:
                nc.vector.tensor_copy(by_slot, values[b][:].indirect(listed))
            words = picked[:].rearrange("p u s v -> p (u s v)").bitcast(F32)
            turned = psum.tile([P, 2, P], F32, name=f"turned{b}{s}")
            for u in range(2):
                nc.tensor.transpose(turned[:, u, :], words[:, u * P : (u + 1) * P], identity[:])
            g = keep.tile([P, P, PACK], BF16, align_bytes=64, name=f"grouped{b}{s}")
            nc.scalar.copy(
                out=g[:].rearrange("p e j -> p (e j)").bitcast(F32).rearrange("p (e u) -> p e u", u=2),
                in_=turned[:].rearrange("p u e -> p e u"),
            )
            grouped[b, s] = g

        def quantize(b, s):
            nc.vector.quantize_mx(
                out=v_codes[s][b][:].bitcast(FP8X4),
                scales=v_scales[s][b][:],
                in_=grouped[b, s][:].rearrange("p e j -> p (e j)"),
            )

        def quantize_weights(s):
            nc.vector.quantize_mx(
                out=w_codes[s][:].bitcast(FP8X4),
                scales=w_scales[s][:],
                in_=w_grouped[s][:].rearrange("p q j -> p (q j)"),
            )

        def round_scalar(s):
            nc.scalar.copy(out=w_grouped[s][:], in_=w_raw[s][:].rearrange("p j q -> p q j"))

        def round_vector(s):
            nc.vector.tensor_copy(out=w_grouped[s][:], in_=w_raw[s][:].rearrange("p j q -> p q j"))

        result = [keep.tile([NQ, DV], F32, name=f"result{s}") for s in range(B)]

        def multiply(s, b):
            acc = psum.tile([NQ, P], F32, name=f"acc{s}{b}")
            nc.tensor.matmul_mx(
                out=acc[:],
                lhsT=w_codes[s][:].bitcast(FP8X4),
                lhsT_scale=w_scales[s][:],
                rhs=v_codes[s][b][:].bitcast(FP8X4),
                rhs_scale=v_scales[s][b][:],
                start=True,
                stop=True,
            )
            return acc

        def finish_scalar(s, b, acc):
            nc.scalar.copy(out=result[s][:, b * P : (b + 1) * P], in_=acc[:])

        def finish_vector(s, b, acc):
            nc.vector.tensor_copy(out=result[s][:, b * P : (b + 1) * P], in_=acc[:])

        def store(s):
            nc.sync.dma_start(out=out[s], in_=result[s][:])

        round_values()
        gather(0, 0)
        gather(0, 1)
        gather(1, 0)
        gather(1, 1)
        round_scalar(0)
        round_vector(1)
        quantize(0, 0)
        quantize(0, 1)
        quantize(1, 0)
        quantize_weights(0)
        quantize_weights(1)
        quantize(1, 1)
        a00 = multiply(0, 0)
        a01 = multiply(0, 1)
        a10 = multiply(1, 0)
        a11 = multiply(1, 1)
        finish_scalar(0, 0, a00)
        finish_scalar(0, 1, a01)
        store(0)
        finish_scalar(1, 0, a10)
        finish_vector(1, 1, a11)
        store(1)
